import numpy as np
import ml_dtypes


def mxq(x, axis, fmt="e4m3"):
    dtype, down = {"e4m3": (ml_dtypes.float8_e4m3fn, 7), "e5m2": (ml_dtypes.float8_e5m2, 14)}[fmt]
    v = np.moveaxis(np.asarray(x, np.float32).astype(ml_dtypes.bfloat16).astype(np.float64), axis, -1)
    blocks = v.reshape(v.shape[:-1] + (-1, 32))
    amax = np.abs(blocks).max(-1, keepdims=True)
    byte = np.maximum(np.where(amax > 0, np.frexp(amax)[1] - 1 + 127, 0) - down, 1)
    scale = np.exp2(byte - 127.0)
    codes = (blocks / scale).astype(np.float32).astype(dtype).astype(np.float64)
    return np.moveaxis((codes * scale).reshape(v.shape), -1, axis)


WIDE = False


def mx_kscale(k):
    if not WIDE:
        return np.ones(k)
    levels = np.array([10, -10, 5, -5, 0])
    if k % 512:
        return np.exp2(np.random.permutation(np.resize(levels, k // 32))).repeat(32)
    a = np.empty((k // 512, 16))
    for p in range(k // 512):
        a[p, :8] = np.random.permutation(np.resize(levels, 8))
        for g in range(8):
            far = levels[np.abs(levels - a[p, g]) >= 10]
            a[p, g + 8] = far[np.random.randint(len(far))]
    return np.exp2(a.ravel()).repeat(32)


def f64(x):
    return np.asarray(x).astype(np.float64)


def striped(idx):
    return np.tile(idx.reshape(-1, 16).T, (8, 1)).astype(np.uint16)


def unstriped(offs):
    return offs[:16].T.reshape(-1).astype(np.int64)


def striped8(idx):
    return np.concatenate([x.reshape(-1, 16).T for x in idx]).astype(np.uint16)


def runs(offs, k):
    lists = np.stack([offs[16 * r : 16 * r + 16].T.reshape(-1) for r in range(8)]).astype(np.int64)
    return lists[np.arange(k) % 512 // 64]


def pack_weight(w):
    k, n = w.shape
    w = f64(np.asarray(w, np.float32).astype(ml_dtypes.bfloat16)).reshape(k // 32, 32, n)
    amax = np.abs(w).max(1)
    byte = np.clip(np.where(amax > 0, np.frexp(amax)[1] - 1 + 127 - 7, 1), 1, 254)
    scaled = (w * np.exp2(127.0 - byte)[:, None, :]).reshape(k, n).astype(np.float32)
    words = np.ascontiguousarray(scaled.reshape(k // 512, 128, 4, n).transpose(0, 1, 3, 2)).astype(ml_dtypes.float8_e4m3fn).view(np.uint8)
    return words, np.ascontiguousarray(byte.astype(np.uint8).reshape(k // 512, 16, n))


def unpack_weight(words, scales):
    g, p, n, _ = words.shape
    vals = np.ascontiguousarray(words).view(ml_dtypes.float8_e4m3fn).astype(np.float64) * np.repeat(np.exp2(scales.astype(np.float64) - 127.0), 8, axis=1)[..., None]
    return vals.transpose(0, 1, 3, 2).reshape(g * 512, n)


K, T, S, N, H, G = 512, 2048, 512, 512, 512, 2048


def setup_inputs():
    n = np.random.standard_normal
    s = mx_kscale(K)[:, None]
    u = mx_kscale(S)
    packed_xT = pack_weight(n((K, T)) * s)
    packed_dT = pack_weight(n((K, G)) / s)
    return {
        "x_words": packed_xT[0],
        "x_scales": packed_xT[1],
        "w1": (n((K, H)) / np.sqrt(K) / s).astype(np.float32),
        "gn": (np.random.uniform(0.5, 1.5, (H, 1)) * u[:, None]).astype(np.float32),
        "w2": (n((H, N)) / np.sqrt(H) / u[:, None]).astype(np.float32),
        "d_words": packed_dT[0],
        "d_scales": packed_dT[1],
        "offs": striped(np.random.permutation(T)[:S]),
        "n1": striped8(np.stack([np.random.permutation(S) for _ in range(8)])),
        "n2": striped8(np.stack([np.random.permutation(S) for _ in range(8)])),
        "two": striped(np.random.permutation(T)[:S]),
        "k1": striped8(np.random.randint(0, G, (8, H))),
        "n3": striped8(np.stack([np.random.permutation(S) for _ in range(8)])),
        "n4": striped8(np.stack([np.random.permutation(S) for _ in range(8)])),
    }


def reference(x_words, x_scales, w1, gn, w2, d_words, d_scales, offs, n1, n2, two, k1, n3, n4):
    xq = unpack_weight(x_words, x_scales)[:, unstriped(offs)]
    y = mxq(f64(w1), 0, "e4m3").T @ xq
    st = np.maximum(y, y[np.arange(H)[:, None], runs(n1, H)])
    z = f64(gn) * (st[np.arange(H)[:, None], runs(n2, H)] - (0.5 * y))
    a = mxq(f64(w2), 0, "e4m3").T @ mxq(z, 0, "e4m3")
    d_k1 = unpack_weight(d_words, d_scales)[np.arange(K)[:, None], runs(k1, K)]
    x_two = unpack_weight(x_words, x_scales)[:, unstriped(two)]
    b = 0.0625 * (d_k1.T @ x_two)
    return a[np.arange(N)[:, None], runs(n3, N)] - (np.tanh(b) * (b[np.arange(H)[:, None], runs(n4, H)]))

@@ -1,0 +1,190 @@
+from contextlib import ExitStack
+
+import concourse.mybir as mybir
+
+F32 = mybir.dt.float32
+BF16 = mybir.dt.bfloat16
+I32 = mybir.dt.int32
+U32 = mybir.dt.uint32
+U16 = mybir.dt.uint16
+U8 = mybir.dt.uint8
+FP8X4 = mybir.dt.float8_e4m3fn_x4
+ALU = mybir.AluOpType
+ACT = mybir.ActivationFunctionType
+
+P = 128
+PACK = 4
+S = 512
+T = 2048
+HALF = S // 2
+LIST_COLS = S // 16
+FLOPS = 3 * 2 * 512 * 512 * 512
+
+
+def tile_picked_cdjoinsoftbhopb_none_p_kernel(
+    tc, x_words, x_scales, w1, gn, w2, d_words, d_scales, offs, n1, n2, two, k1, n3, n4, out
+):
+    nc = tc.nc
+    with ExitStack() as ctx:
+        keep = ctx.enter_context(tc.tile_pool(name="keep", bufs=1))
+        psum = ctx.enter_context(tc.psum_pool(name="psum", bufs=1))
+
+        def tile(name, shape, dtype):
+            return keep.tile(shape, dtype, name=name, align_bytes=64)
+
+        def load_list(name, source):
+            held = tile(name, [P, LIST_COLS], U16)
+            nc.sync.dma_start(held[:], source)
+            return held
+
+        def load_words(name, source):
+            held = tile(name, [P, T], I32)
+            nc.sync.dma_start(held[:], source[0].rearrange("p n r -> p (n r)").bitcast(I32))
+            return held
+
+        def cols(h):
+            return slice(h * HALF, (h + 1) * HALF)
+
+        def half_list(held, h):
+            return held[:, h * LIST_COLS // 2 : (h + 1) * LIST_COLS // 2]
+
+        x_bytes = tile("x_bytes", [P, T], U8)
+        d_bytes = tile("d_bytes", [P, T], U8)
+        nc.vector.memset(x_bytes[:].bitcast(I32), 0)
+        nc.vector.memset(d_bytes[:].bitcast(I32), 0)
+
+        offs_l = load_list("offs_l", offs)
+        w1_rows = w1.rearrange("(p j) c -> p j c", j=PACK)
+        w1_raw = [tile("w1_raw%d" % h, [P, PACK, HALF], F32) for h in range(2)]
+        nc.sync.dma_start(w1_raw[0][:], w1_rows[:, :, cols(0)])
+        for s in range(4):
+            nc.sync.dma_start(x_bytes[s:P:32, :].bitcast(I32), x_scales[0, s:16:4, :].bitcast(I32))
+        nc.sync.dma_start(w1_raw[1][:], w1_rows[:, :, cols(1)])
+        x_table = load_words("x_table", x_words)
+        two_l = load_list("two_l", two)
+        k1_l = load_list("k1_l", k1)
+        for e in range(2):
+            nc.sync.dma_start(d_bytes[e:P:16, :].bitcast(I32), d_scales[0, e:16:2, :].bitcast(I32))
+        d_table = load_words("d_table", d_words)
+        n1_l = load_list("n1_l", n1)
+        n2_l = load_list("n2_l", n2)
+        gain = tile("gain", [P, PACK], F32)
+        nc.sync.dma_start(gain[:], gn.rearrange("(p t) o -> p (t o)", t=PACK))
+        w2_raw = tile("w2_raw", [P, PACK, S], F32)
+        nc.sync.dma_start(w2_raw[:], w2.rearrange("(p j) c -> p j c", j=PACK))
+        n4_l = load_list("n4_l", n4)
+        n3_l = load_list("n3_l", n3)
+
+        def pick(name, table, held, dtype):
+            picked = tile(name, [P, S], dtype)
+            nc.vector.tensor_copy(picked[:], table[:].bitcast(dtype).indirect(held[:]))
+            return picked
+
+        def pick_bytes(name, table, held):
+            picked = tile(name, [P, S], U8)
+            nc.vector.tensor_copy(picked[:], table[:].indirect(held[:]))
+            return picked
+
+        def quantise(name, grouped, width):
+            codes = tile(name + "_codes", [P, width], U32)
+            scales = tile(name + "_scales", [P, width], U8)
+            nc.vector.quantize_mx(out=codes[:].bitcast(FP8X4), scales=scales[:], in_=grouped)
+            return codes, scales
+
+        def product(acc, lhs, t, rhs):
+            m = slice(t * P, (t + 1) * P)
+            nc.tensor.matmul_mx(
+                out=acc, lhsT=lhs[0][:, m].bitcast(FP8X4), lhsT_scale=lhs[1][:, m],
+                rhs=rhs[0][:].bitcast(FP8X4), rhs_scale=rhs[1][:], start=True, stop=True,
+            )
+
+        xo_bytes = pick_bytes("xo_bytes", x_bytes, offs_l)
+        w1_grouped = tile("w1_grouped", [P, PACK, P, PACK], BF16)
+        for h in range(2):
+            nc.scalar.copy(
+                w1_grouped[:, :, h * 64 : (h + 1) * 64, :].rearrange("p t m j -> p m j t"),
+                w1_raw[h][:].rearrange("p j (m t) -> p m j t", t=PACK),
+            )
+        w1_q = quantise("w1", w1_grouped[:].rearrange("p t m j -> p (t m j)"), S)
+        xo_words = pick("xo_words", x_table, offs_l, U32)
+
+        xt_bytes = pick_bytes("xt_bytes", x_bytes, two_l)
+        dk_bytes = pick_bytes("dk_bytes", d_bytes, k1_l)
+        dealt_bytes = tile("dealt_bytes", [P, S], U8)
+        nc.vector.tensor_copy(
+            dealt_bytes[:].rearrange("p (t m) -> p m t", t=PACK), dk_bytes[:].rearrange("p (m t) -> p m t", t=PACK)
+        )
+        for e in range(2):
+            nc.sync.dma_start(dealt_bytes[2 + e : P : 32, :].bitcast(I32), dealt_bytes[16 + e : P : 32, :].bitcast(I32))
+        xt_words = pick("xt_words", x_table, two_l, U32)
+        dk_words = pick("dk_words", d_table, k1_l, U32)
+        dealt_words = tile("dealt_words", [P, S], U32)
+        nc.vector.tensor_copy(
+            dealt_words[:].rearrange("p (t m) -> p m t", t=PACK), dk_words[:].rearrange("p (m t) -> p m t", t=PACK)
+        )
+
+        z_planes = tile("z_planes", [P, PACK, S], BF16)
+        for t in range(PACK):
+            y_acc = psum.tile([P, S], F32, name="ya_acc%d" % t)
+            product(y_acc[:], w1_q, t, (xo_words, xo_bytes))
+            y = tile("y%d" % t, [P, S], F32)
+            nc.scalar.copy(y[:], y_acc[:])
+            y_n1 = tile("y_n1_%d" % t, [P, S], F32)
+            st2 = tile("st2_%d" % t, [P, S], F32)
+            diff = tile("diff%d" % t, [P, S], F32)
+            for h in range(2):
+                nc.scalar.activation(y_n1[:, cols(h)], y[:].indirect(half_list(n1_l, h)), ACT.Copy, scale=2.0)
+            nc.vector.scalar_tensor_tensor(st2[:], y[:], 2.0, y_n1[:], ALU.mult, ALU.max)
+            for h in range(2):
+                nc.vector.tensor_tensor(diff[:, cols(h)], st2[:].indirect(half_list(n2_l, h)), y[:, cols(h)], ALU.subtract)
+            nc.vector.tensor_scalar(z_planes[:, t, :], diff[:], gain[:, t : t + 1], 0.5, ALU.mult, ALU.mult)
+
+        w2_grouped = tile("w2_grouped", [P, PACK, P, PACK], BF16)
+        nc.vector.tensor_copy(
+            w2_grouped[:].rearrange("p t m j -> p m j t"), w2_raw[:].rearrange("p j (m t) -> p m j t", t=PACK)
+        )
+        w2_q = quantise("w2", w2_grouped[:].rearrange("p t m j -> p (t m j)"), S)
+
+        z_q = []
+        for h in range(2):
+            z_grouped = tile("z_grouped%d" % h, [P, HALF, PACK], BF16)
+            nc.vector.tensor_copy(
+                z_grouped[:].rearrange("p (c i) t -> p c t i", i=4),
+                z_planes[:, :, cols(h)].rearrange("p t (c i) -> p c t i", i=4),
+            )
+            z_q.append(quantise("z%d" % h, z_grouped[:].rearrange("p c t -> p (c t)"), HALF))
+
+        mixed = []
+        for t in range(PACK):
+            b_acc = psum.tile([P, S], F32, name="b_acc%d" % t)
+            product(b_acc[:], (dealt_words, dealt_bytes), t, (xt_words, xt_bytes))
+            b = tile("b%d" % t, [P, S], F32)
+            nc.scalar.activation(b[:], b_acc[:], ACT.Copy, scale=0.0625)
+            tanh_b = tile("tanh_b%d" % t, [P, S], F32)
+            nc.scalar.activation(tanh_b[:], b_acc[:], ACT.Tanh, scale=0.0625)
+            b_n4 = tile("b_n4_%d" % t, [P, S], F32)
+            for h in range(2):
+                nc.scalar.activation(b_n4[:, cols(h)], b[:].indirect(half_list(n4_l, h)), ACT.Copy)
+            mix = tile("mix%d" % t, [P, S], F32)
+            nc.vector.tensor_tensor(mix[:], b_n4[:], tanh_b[:], ALU.mult)
+            mixed.append(mix)
+
+        out_rows = out.rearrange("(p t) j -> t p j", t=PACK)
+        for t in range(PACK):
+            a_acc = psum.tile([P, S], F32, name="ya_acc%d" % t)
+            a = tile("a%d" % t, [P, S], F32)
+            for h in range(2):
+                product(a_acc[:, cols(h)], w2_q, t, z_q[h])
+            nc.scalar.copy(a[:], a_acc[:])
+            result = tile("result%d" % t, [P, S], F32)
+            if t % 2 == 0:
+                for h in range(2):
+                    nc.vector.tensor_tensor(
+                        result[:, cols(h)], a[:].indirect(half_list(n3_l, h)), mixed[t][:, cols(h)], ALU.subtract
+                    )
+            else:
+                a_n3 = tile("a_n3_%d" % t, [P, S], F32)
+                for h in range(2):
+                    nc.scalar.activation(a_n3[:, cols(h)], a[:].indirect(half_list(n3_l, h)), ACT.Copy)
+                nc.vector.tensor_tensor(result[:], a_n3[:], mixed[t][:], ALU.subtract)
+            nc.sync.dma_start(out_rows[t], result[:])

@@ -27,6 +27,7 @@ def tile_picked_cdjoinsoftbhopb_none_p_kernel(
     nc = tc.nc
     with ExitStack() as ctx:
         keep = ctx.enter_context(tc.tile_pool(name="keep", bufs=1))
+        shared = ctx.enter_context(tc.tile_pool(name="shared", bufs=1))
         psum = ctx.enter_context(tc.psum_pool(name="psum", bufs=1))
 
         def tile(name, shape, dtype):
@@ -59,31 +60,34 @@ def tile_picked_cdjoinsoftbhopb_none_p_kernel(
         nc.sync.dma_start(w1_raw[0][:], w1_rows[:, :, cols(0)])
         for s in range(4):
             nc.sync.dma_start(x_bytes[s:P:32, :].bitcast(I32), x_scales[0, s:16:4, :].bitcast(I32))
+        two_l = load_list("two_l", two)
         nc.sync.dma_start(w1_raw[1][:], w1_rows[:, :, cols(1)])
         x_table = load_words("x_table", x_words)
-        two_l = load_list("two_l", two)
         k1_l = load_list("k1_l", k1)
         for e in range(2):
             nc.sync.dma_start(d_bytes[e:P:16, :].bitcast(I32), d_scales[0, e:16:2, :].bitcast(I32))
-        d_table = load_words("d_table", d_words)
         n1_l = load_list("n1_l", n1)
         n2_l = load_list("n2_l", n2)
         gain = tile("gain", [P, PACK], F32)
         nc.sync.dma_start(gain[:], gn.rearrange("(p t) o -> p (t o)", t=PACK))
+        d_table = shared.tile([P, T], I32, name="d_table", align_bytes=64, offset=0)
+        nc.sync.dma_start(d_table[:], d_words[0].rearrange("p n r -> p (n r)").bitcast(I32))
         w2_raw = tile("w2_raw", [P, PACK, S], F32)
         nc.sync.dma_start(w2_raw[:], w2.rearrange("(p j) c -> p j c", j=PACK))
         n4_l = load_list("n4_l", n4)
         n3_l = load_list("n3_l", n3)
 
-        def pick(name, table, held, dtype):
+        def pick(name, window, held, dtype):
             picked = tile(name, [P, S], dtype)
-            nc.vector.tensor_copy(picked[:], table[:].bitcast(dtype).indirect(held[:]))
+            nc.vector.tensor_copy(picked[:], window.indirect(held[:]))
             return picked
 
-        def pick_bytes(name, table, held):
-            picked = tile(name, [P, S], U8)
-            nc.vector.tensor_copy(picked[:], table[:].indirect(held[:]))
-            return picked
+        def deal(name, picked, dtype):
+            dealt = tile(name, [P, S], dtype)
+            nc.vector.tensor_copy(
+                dealt[:].rearrange("p (t m) -> p m t", t=PACK), picked[:].rearrange("p (m t) -> p m t", t=PACK)
+            )
+            return dealt
 
         def quantise(name, grouped, width):
             codes = tile(name + "_codes", [P, width], U32)
@@ -98,7 +102,11 @@ def tile_picked_cdjoinsoftbhopb_none_p_kernel(
                 rhs=rhs[0][:].bitcast(FP8X4), rhs_scale=rhs[1][:], start=True, stop=True,
             )
 
-        xo_bytes = pick_bytes("xo_bytes", x_bytes, offs_l)
+        def planes(name, dtype=F32):
+            return [tile("%s%d" % (name, t), [P, S], dtype) for t in range(PACK)]
+
+        xo_bytes = pick("xo_bytes", x_bytes[:], offs_l, U8)
+        xt_bytes = pick("xt_bytes", x_bytes[:], two_l, U8)
         w1_grouped = tile("w1_grouped", [P, PACK, P, PACK], BF16)
         for h in range(2):
             nc.scalar.copy(
@@ -106,85 +114,99 @@ def tile_picked_cdjoinsoftbhopb_none_p_kernel(
                 w1_raw[h][:].rearrange("p j (m t) -> p m j t", t=PACK),
             )
         w1_q = quantise("w1", w1_grouped[:].rearrange("p t m j -> p (t m j)"), S)
-        xo_words = pick("xo_words", x_table, offs_l, U32)
-
-        xt_bytes = pick_bytes("xt_bytes", x_bytes, two_l)
-        dk_bytes = pick_bytes("dk_bytes", d_bytes, k1_l)
-        dealt_bytes = tile("dealt_bytes", [P, S], U8)
-        nc.vector.tensor_copy(
-            dealt_bytes[:].rearrange("p (t m) -> p m t", t=PACK), dk_bytes[:].rearrange("p (m t) -> p m t", t=PACK)
-        )
+        xo_words = pick("xo_words", x_table[:].bitcast(U32), offs_l, U32)
+        dk_bytes = pick("dk_bytes", d_bytes[:], k1_l, U8)
+        xt_words = pick("xt_words", x_table[:].bitcast(U32), two_l, U32)
+        dealt_bytes = deal("dealt_bytes", dk_bytes, U8)
         for e in range(2):
             nc.sync.dma_start(dealt_bytes[2 + e : P : 32, :].bitcast(I32), dealt_bytes[16 + e : P : 32, :].bitcast(I32))
-        xt_words = pick("xt_words", x_table, two_l, U32)
-        dk_words = pick("dk_words", d_table, k1_l, U32)
-        dealt_words = tile("dealt_words", [P, S], U32)
-        nc.vector.tensor_copy(
-            dealt_words[:].rearrange("p (t m) -> p m t", t=PACK), dk_words[:].rearrange("p (m t) -> p m t", t=PACK)
-        )
 
+        y, y_n1, diff = planes("y"), planes("y_n1"), planes("diff")
+        st2 = [shared.tile([P, S], F32, name="st2_%d" % t, align_bytes=64, offset=t * S * 4) for t in range(PACK)]
         z_planes = tile("z_planes", [P, PACK, S], BF16)
-        for t in range(PACK):
+
+        def project(t):
             y_acc = psum.tile([P, S], F32, name="ya_acc%d" % t)
             product(y_acc[:], w1_q, t, (xo_words, xo_bytes))
-            y = tile("y%d" % t, [P, S], F32)
-            nc.scalar.copy(y[:], y_acc[:])
-            y_n1 = tile("y_n1_%d" % t, [P, S], F32)
-            st2 = tile("st2_%d" % t, [P, S], F32)
-            diff = tile("diff%d" % t, [P, S], F32)
-            for h in range(2):
-                nc.scalar.activation(y_n1[:, cols(h)], y[:].indirect(half_list(n1_l, h)), ACT.Copy, scale=2.0)
-            nc.vector.scalar_tensor_tensor(st2[:], y[:], 2.0, y_n1[:], ALU.mult, ALU.max)
-            for h in range(2):
-                nc.vector.tensor_tensor(diff[:, cols(h)], st2[:].indirect(half_list(n2_l, h)), y[:, cols(h)], ALU.subtract)
-            nc.vector.tensor_scalar(z_planes[:, t, :], diff[:], gain[:, t : t + 1], 0.5, ALU.mult, ALU.mult)
+            nc.scalar.copy(y[t][:], y_acc[:])
 
+        def fetch_n1(t):
+            for h in range(2):
+                nc.scalar.activation(y_n1[t][:, cols(h)], y[t][:].indirect(half_list(n1_l, h)), ACT.Copy, scale=2.0)
+
+        def larger(t):
+            nc.vector.scalar_tensor_tensor(st2[t][:], y[t][:], 2.0, y_n1[t][:], ALU.mult, ALU.max)
+
+        def fetch_n2(t, h):
+            nc.vector.tensor_tensor(
+                diff[t][:, cols(h)], st2[t][:].indirect(half_list(n2_l, h)), y[t][:, cols(h)], ALU.subtract
+            )
+
+        def apply_gain(t, c):
+            nc.vector.tensor_scalar(z_planes[:, t, c], diff[t][:, c], gain[:, t : t + 1], 0.5, ALU.mult, ALU.mult)
+
+        project(0)
+        for t in range(PACK):
+            if t + 1 < PACK:
+                project(t + 1)
+            fetch_n1(t)
+
+        dk_words = pick("dk_words", d_table[:].bitcast(U32), k1_l, U32)
+        larger(0)
+        dealt_words = deal("dealt_words", dk_words, U32)
+        fetch_n2(0, 0)
+        fetch_n2(0, 1)
+        for t in range(1, PACK):
+            larger(t)
+            apply_gain(t - 1, slice(0, S))
+            fetch_n2(t, 0)
+            fetch_n2(t, 1)
         w2_grouped = tile("w2_grouped", [P, PACK, P, PACK], BF16)
         nc.vector.tensor_copy(
             w2_grouped[:].rearrange("p t m j -> p m j t"), w2_raw[:].rearrange("p j (m t) -> p m j t", t=PACK)
         )
+        apply_gain(PACK - 1, slice(0, S))
         w2_q = quantise("w2", w2_grouped[:].rearrange("p t m j -> p (t m j)"), S)
-
-        z_q = []
+        z_grouped = [tile("z_grouped%d" % h, [P, HALF, PACK], BF16) for h in range(2)]
         for h in range(2):
-            z_grouped = tile("z_grouped%d" % h, [P, HALF, PACK], BF16)
             nc.vector.tensor_copy(
-                z_grouped[:].rearrange("p (c i) t -> p c t i", i=4),
+                z_grouped[h][:].rearrange("p (c i) t -> p c t i", i=4),
                 z_planes[:, :, cols(h)].rearrange("p t (c i) -> p c t i", i=4),
             )
-            z_q.append(quantise("z%d" % h, z_grouped[:].rearrange("p c t -> p (c t)"), HALF))
+        z_q = [quantise("z%d" % h, z_grouped[h][:].rearrange("p c t -> p (c t)"), HALF) for h in range(2)]
 
-        mixed = []
+        b, tanh_b, b_n4, mix, a = planes("b"), planes("tanh_b"), planes("b_n4"), planes("mix"), planes("a")
         for t in range(PACK):
             b_acc = psum.tile([P, S], F32, name="b_acc%d" % t)
             product(b_acc[:], (dealt_words, dealt_bytes), t, (xt_words, xt_bytes))
-            b = tile("b%d" % t, [P, S], F32)
-            nc.scalar.activation(b[:], b_acc[:], ACT.Copy, scale=0.0625)
-            tanh_b = tile("tanh_b%d" % t, [P, S], F32)
-            nc.scalar.activation(tanh_b[:], b_acc[:], ACT.Tanh, scale=0.0625)
-            b_n4 = tile("b_n4_%d" % t, [P, S], F32)
+            nc.scalar.activation(b[t][:], b_acc[:], ACT.Copy, scale=0.0625)
+            nc.scalar.activation(tanh_b[t][:], b_acc[:], ACT.Tanh, scale=0.0625)
+            if t in ():
+                for h in range(2):
+                    nc.vector.tensor_tensor(
+                        mix[t][:, cols(h)], b[t][:].indirect(half_list(n4_l, h)), tanh_b[t][:, cols(h)], ALU.mult
+                    )
+            else:
+                for h in range(2):
+                    nc.scalar.activation(b_n4[t][:, cols(h)], b[t][:].indirect(half_list(n4_l, h)), ACT.Copy)
+                nc.vector.tensor_tensor(mix[t][:], b_n4[t][:], tanh_b[t][:], ALU.mult)
+
+        for t in range(PACK):
+            a_acc = psum.tile([P, S], F32, name="ya_acc%d" % t)
             for h in range(2):
-                nc.scalar.activation(b_n4[:, cols(h)], b[:].indirect(half_list(n4_l, h)), ACT.Copy)
-            mix = tile("mix%d" % t, [P, S], F32)
-            nc.vector.tensor_tensor(mix[:], b_n4[:], tanh_b[:], ALU.mult)
-            mixed.append(mix)
+                product(a_acc[:, cols(h)], w2_q, t, z_q[h])
+            nc.scalar.copy(a[t][:], a_acc[:])
 
         out_rows = out.rearrange("(p t) j -> t p j", t=PACK)
         for t in range(PACK):
-            a_acc = psum.tile([P, S], F32, name="ya_acc%d" % t)
-            a = tile("a%d" % t, [P, S], F32)
             for h in range(2):
-                product(a_acc[:, cols(h)], w2_q, t, z_q[h])
-            nc.scalar.copy(a[:], a_acc[:])
-            result = tile("result%d" % t, [P, S], F32)
-            if t % 2 == 0:
-                for h in range(2):
+                result = tile("result%d_%d" % (t, h), [P, HALF], F32)
+                if t in (0, 1, 2):
                     nc.vector.tensor_tensor(
-                        result[:, cols(h)], a[:].indirect(half_list(n3_l, h)), mixed[t][:, cols(h)], ALU.subtract
+                        result[:], a[t][:].indirect(half_list(n3_l, h)), mix[t][:, cols(h)], ALU.subtract
                     )
-            else:
-                a_n3 = tile("a_n3_%d" % t, [P, S], F32)
-                for h in range(2):
-                    nc.scalar.activation(a_n3[:, cols(h)], a[:].indirect(half_list(n3_l, h)), ACT.Copy)
-                nc.vector.tensor_tensor(result[:], a_n3[:], mixed[t][:], ALU.subtract)
-            nc.sync.dma_start(out_rows[t], result[:])
+                else:
+                    a_n3 = tile("a_n3_%d_%d" % (t, h), [P, HALF], F32)
+                    nc.scalar.activation(a_n3[:], a[t][:].indirect(half_list(n3_l, h)), ACT.Copy)
+                    nc.vector.tensor_tensor(result[:], a_n3[:], mix[t][:, cols(h)], ALU.subtract)
+                nc.sync.dma_start(out_rows[t][:, cols(h)], result[:])

@@ -125,17 +125,18 @@ def tile_picked_cdjoinsoftbhopb_none_p_kernel(
         st2 = [shared.tile([P, S], F32, name="st2_%d" % t, align_bytes=64, offset=t * S * 4) for t in range(PACK)]
         z_planes = tile("z_planes", [P, PACK, S], BF16)
 
+        y_acc = [psum.tile([P, S], F32, name="ya_acc%d" % t) for t in range(PACK)]
+
         def project(t):
-            y_acc = psum.tile([P, S], F32, name="ya_acc%d" % t)
-            product(y_acc[:], w1_q, t, (xo_words, xo_bytes))
-            nc.scalar.copy(y[t][:], y_acc[:])
+            product(y_acc[t][:], w1_q, t, (xo_words, xo_bytes))
+            nc.scalar.copy(y[t][:], y_acc[t][:])
 
         def fetch_n1(t):
             for h in range(2):
                 nc.scalar.activation(y_n1[t][:, cols(h)], y[t][:].indirect(half_list(n1_l, h)), ACT.Copy, scale=2.0)
 
         def larger(t):
-            nc.vector.scalar_tensor_tensor(st2[t][:], y[t][:], 2.0, y_n1[t][:], ALU.mult, ALU.max)
+            nc.vector.scalar_tensor_tensor(st2[t][:], y_acc[t][:], 2.0, y_n1[t][:], ALU.mult, ALU.max)
 
         def fetch_n2(t, h):
             nc.vector.tensor_tensor(
@@ -201,7 +202,7 @@ def tile_picked_cdjoinsoftbhopb_none_p_kernel(
         for t in range(PACK):
             for h in range(2):
                 result = tile("result%d_%d" % (t, h), [P, HALF], F32)
-                if t in (0, 1, 2):
+                if 2 * t + h < 5:
                     nc.vector.tensor_tensor(
                         result[:], a[t][:].indirect(half_list(n3_l, h)), mix[t][:, cols(h)], ALU.subtract
                     )

@@ -18,6 +18,7 @@ S = 512
 T = 2048
 HALF = S // 2
 LIST_COLS = S // 16
+EARLY = 192
 FLOPS = 3 * 2 * 512 * 512 * 512
 
 
@@ -28,6 +29,7 @@ def tile_picked_cdjoinsoftbhopb_none_p_kernel(
     with ExitStack() as ctx:
         keep = ctx.enter_context(tc.tile_pool(name="keep", bufs=1))
         shared = ctx.enter_context(tc.tile_pool(name="shared", bufs=1))
+        staged = ctx.enter_context(tc.tile_pool(name="staged", bufs=1))
         psum = ctx.enter_context(tc.psum_pool(name="psum", bufs=1))
 
         def tile(name, shape, dtype):
@@ -67,13 +69,16 @@ def tile_picked_cdjoinsoftbhopb_none_p_kernel(
         for e in range(2):
             nc.sync.dma_start(d_bytes[e:P:16, :].bitcast(I32), d_scales[0, e:16:2, :].bitcast(I32))
         n1_l = load_list("n1_l", n1)
+        w2_rows = w2.rearrange("(p j) c -> p j c", j=PACK)
+        w2_early = staged.tile([P, PACK, S], F32, name="w2_early", align_bytes=64, offset=0)
+        nc.sync.dma_start(w2_early[:, :, 0:EARLY], w2_rows[:, :, 0:EARLY])
+        d_table = shared.tile([P, T], I32, name="d_table", align_bytes=64, offset=0)
+        nc.sync.dma_start(d_table[:], d_words[0].rearrange("p n r -> p (n r)").bitcast(I32))
         n2_l = load_list("n2_l", n2)
         gain = tile("gain", [P, PACK], F32)
         nc.sync.dma_start(gain[:], gn.rearrange("(p t) o -> p (t o)", t=PACK))
-        d_table = shared.tile([P, T], I32, name="d_table", align_bytes=64, offset=0)
-        nc.sync.dma_start(d_table[:], d_words[0].rearrange("p n r -> p (n r)").bitcast(I32))
-        w2_raw = tile("w2_raw", [P, PACK, S], F32)
-        nc.sync.dma_start(w2_raw[:], w2.rearrange("(p j) c -> p j c", j=PACK))
+        w2_late = tile("w2_late", [P, PACK, S - EARLY], F32)
+        nc.sync.dma_start(w2_late[:], w2_rows[:, :, EARLY:S])
         n4_l = load_list("n4_l", n4)
         n3_l = load_list("n3_l", n3)
 
@@ -121,7 +126,13 @@ def tile_picked_cdjoinsoftbhopb_none_p_kernel(
         for e in range(2):
             nc.sync.dma_start(dealt_bytes[2 + e : P : 32, :].bitcast(I32), dealt_bytes[16 + e : P : 32, :].bitcast(I32))
 
-        y, y_n1, diff = planes("y"), planes("y_n1"), planes("diff")
+        w2_grouped = tile("w2_grouped", [P, PACK, P, PACK], BF16)
+        nc.scalar.copy(
+            w2_grouped[:, :, 0 : EARLY // PACK, :].rearrange("p t m j -> p m j t"),
+            w2_early[:, :, 0:EARLY].rearrange("p j (m t) -> p m j t", t=PACK),
+        )
+        y_n1, diff = planes("y_n1"), planes("diff")
+        y = [staged.tile([P, S], F32, name="y%d" % t, align_bytes=64, offset=t * S * 4) for t in range(PACK)]
         st2 = [shared.tile([P, S], F32, name="st2_%d" % t, align_bytes=64, offset=t * S * 4) for t in range(PACK)]
         z_planes = tile("z_planes", [P, PACK, S], BF16)
 
@@ -162,9 +173,9 @@ def tile_picked_cdjoinsoftbhopb_none_p_kernel(
             apply_gain(t - 1, slice(0, S))
             fetch_n2(t, 0)
             fetch_n2(t, 1)
-        w2_grouped = tile("w2_grouped", [P, PACK, P, PACK], BF16)
         nc.vector.tensor_copy(
-            w2_grouped[:].rearrange("p t m j -> p m j t"), w2_raw[:].rearrange("p j (m t) -> p m j t", t=PACK)
+            w2_grouped[:, :, EARLY // PACK : P, :].rearrange("p t m j -> p m j t"),
+            w2_late[:].rearrange("p j (m t) -> p m j t", t=PACK),
         )
         apply_gain(PACK - 1, slice(0, S))
         w2_q = quantise("w2", w2_grouped[:].rearrange("p t m j -> p (t m j)"), S)
@@ -182,15 +193,18 @@ def tile_picked_cdjoinsoftbhopb_none_p_kernel(
             product(b_acc[:], (dealt_words, dealt_bytes), t, (xt_words, xt_bytes))
             nc.scalar.activation(b[t][:], b_acc[:], ACT.Copy, scale=0.0625)
             nc.scalar.activation(tanh_b[t][:], b_acc[:], ACT.Tanh, scale=0.0625)
-            if t in ():
-                for h in range(2):
+            plain = [h for h in range(2) if 2 * t + h < 5]
+            for h in range(2):
+                if h in plain:
+                    nc.scalar.activation(b_n4[t][:, cols(h)], b[t][:].indirect(half_list(n4_l, h)), ACT.Copy)
+            if plain:
+                span = slice(0, HALF * len(plain))
+                nc.vector.tensor_tensor(mix[t][:, span], b_n4[t][:, span], tanh_b[t][:, span], ALU.mult)
+            for h in range(2):
+                if h not in plain:
                     nc.vector.tensor_tensor(
                         mix[t][:, cols(h)], b[t][:].indirect(half_list(n4_l, h)), tanh_b[t][:, cols(h)], ALU.mult
                     )
-            else:
-                for h in range(2):
-                    nc.scalar.activation(b_n4[t][:, cols(h)], b[t][:].indirect(half_list(n4_l, h)), ACT.Copy)
-                nc.vector.tensor_tensor(mix[t][:], b_n4[t][:], tanh_b[t][:], ALU.mult)
 
         for t in range(PACK):
             a_acc = psum.tile([P, S], F32, name="ya_acc%d" % t)
@@ -202,7 +216,7 @@ def tile_picked_cdjoinsoftbhopb_none_p_kernel(
         for t in range(PACK):
             for h in range(2):
                 result = tile("result%d_%d" % (t, h), [P, HALF], F32)
-                if 2 * t + h < 5:
+                if 2 * t + h < 4:
                     nc.vector.tensor_tensor(
                         result[:], a[t][:].indirect(half_list(n3_l, h)), mix[t][:, cols(h)], ALU.subtract
                     )

@@ -17,8 +17,13 @@ PACK = 4
 S = 512
 T = 2048
 HALF = S // 2
-LIST_COLS = S // 16
-EARLY = 192
+GROUP = 16
+QUADRANT = 32
+BLOCKS = 16
+F32_BYTES = 4
+WINDOW = 2 * S
+W2_ON_SCALAR = 192
+FUSED_HALVES = 5
 FLOPS = 3 * 2 * 512 * 512 * 512
 
 
@@ -28,63 +33,68 @@ def tile_picked_cdjoinsoftbhopb_none_p_kernel(
     nc = tc.nc
     with ExitStack() as ctx:
         keep = ctx.enter_context(tc.tile_pool(name="keep", bufs=1))
-        shared = ctx.enter_context(tc.tile_pool(name="shared", bufs=1))
-        staged = ctx.enter_context(tc.tile_pool(name="staged", bufs=1))
+        d_then_st = ctx.enter_context(tc.tile_pool(name="d_then_st", bufs=1))
+        w2_then_y = ctx.enter_context(tc.tile_pool(name="w2_then_y", bufs=1))
         psum = ctx.enter_context(tc.psum_pool(name="psum", bufs=1))
 
         def tile(name, shape, dtype):
             return keep.tile(shape, dtype, name=name, align_bytes=64)
 
-        def load_list(name, source):
-            held = tile(name, [P, LIST_COLS], U16)
-            nc.sync.dma_start(held[:], source)
-            return held
+        def planes(name, width):
+            return [tile("%s%d" % (name, t), [P, width], F32) for t in range(PACK)]
 
-        def load_words(name, source):
-            held = tile(name, [P, T], I32)
-            nc.sync.dma_start(held[:], source[0].rearrange("p n r -> p (n r)").bitcast(I32))
-            return held
+        def windows(pool, name):
+            return [
+                pool.tile([P, WINDOW], F32, name="%s%d" % (name, t), align_bytes=64, offset=t * WINDOW * F32_BYTES)
+                for t in range(PACK)
+            ]
 
-        def cols(h):
+        def half(h):
             return slice(h * HALF, (h + 1) * HALF)
 
-        def half_list(held, h):
-            return held[:, h * LIST_COLS // 2 : (h + 1) * LIST_COLS // 2]
+        def load_list(name, source):
+            offsets = tile(name, [P, S // GROUP], U16)
+            nc.sync.dma_start(offsets[:], source)
+            return offsets
+
+        def as_words(packed):
+            return packed[0].rearrange("p n r -> p (n r)").bitcast(I32)
 
         x_bytes = tile("x_bytes", [P, T], U8)
         d_bytes = tile("d_bytes", [P, T], U8)
         nc.vector.memset(x_bytes[:].bitcast(I32), 0)
         nc.vector.memset(d_bytes[:].bitcast(I32), 0)
 
-        offs_l = load_list("offs_l", offs)
+        offs_list = load_list("offs_list", offs)
         w1_rows = w1.rearrange("(p j) c -> p j c", j=PACK)
         w1_raw = [tile("w1_raw%d" % h, [P, PACK, HALF], F32) for h in range(2)]
-        nc.sync.dma_start(w1_raw[0][:], w1_rows[:, :, cols(0)])
-        for s in range(4):
-            nc.sync.dma_start(x_bytes[s:P:32, :].bitcast(I32), x_scales[0, s:16:4, :].bitcast(I32))
-        two_l = load_list("two_l", two)
-        nc.sync.dma_start(w1_raw[1][:], w1_rows[:, :, cols(1)])
-        x_table = load_words("x_table", x_words)
-        k1_l = load_list("k1_l", k1)
+        nc.sync.dma_start(w1_raw[0][:], w1_rows[:, :, half(0)])
+        for s in range(PACK):
+            nc.sync.dma_start(x_bytes[s:P:QUADRANT, :].bitcast(I32), x_scales[0, s:BLOCKS:PACK, :].bitcast(I32))
+        two_list = load_list("two_list", two)
+        nc.sync.dma_start(w1_raw[1][:], w1_rows[:, :, half(1)])
+        x_table = tile("x_table", [P, T], I32)
+        nc.sync.dma_start(x_table[:], as_words(x_words))
+        k1_list = load_list("k1_list", k1)
         for e in range(2):
-            nc.sync.dma_start(d_bytes[e:P:16, :].bitcast(I32), d_scales[0, e:16:2, :].bitcast(I32))
-        n1_l = load_list("n1_l", n1)
+            nc.sync.dma_start(d_bytes[e:P:GROUP, :].bitcast(I32), d_scales[0, e:BLOCKS:2, :].bitcast(I32))
+        n1_list = load_list("n1_list", n1)
         w2_rows = w2.rearrange("(p j) c -> p j c", j=PACK)
-        w2_early = staged.tile([P, PACK, S], F32, name="w2_early", align_bytes=64, offset=0)
-        nc.sync.dma_start(w2_early[:, :, 0:EARLY], w2_rows[:, :, 0:EARLY])
-        d_table = shared.tile([P, T], I32, name="d_table", align_bytes=64, offset=0)
-        nc.sync.dma_start(d_table[:], d_words[0].rearrange("p n r -> p (n r)").bitcast(I32))
-        n2_l = load_list("n2_l", n2)
+        w2_first = w2_then_y.tile([P, PACK, WINDOW], F32, name="w2_first", align_bytes=64, offset=0)
+        nc.sync.dma_start(w2_first[:, :, 0:W2_ON_SCALAR], w2_rows[:, :, 0:W2_ON_SCALAR])
+        d_table = d_then_st.tile([P, T], I32, name="d_table", align_bytes=64, offset=S * F32_BYTES)
+        nc.sync.dma_start(d_table[:], as_words(d_words))
+        n2_list = load_list("n2_list", n2)
         gain = tile("gain", [P, PACK], F32)
         nc.sync.dma_start(gain[:], gn.rearrange("(p t) o -> p (t o)", t=PACK))
-        w2_late = tile("w2_late", [P, PACK, S - EARLY], F32)
-        nc.sync.dma_start(w2_late[:], w2_rows[:, :, EARLY:S])
-        n4_l = load_list("n4_l", n4)
-        n3_l = load_list("n3_l", n3)
+        w2_rest = tile("w2_rest", [P, PACK, S - W2_ON_SCALAR], F32)
+        nc.sync.dma_start(w2_rest[:], w2_rows[:, :, W2_ON_SCALAR:S])
+        n4_list = load_list("n4_list", n4)
+        n3_list = load_list("n3_list", n3)
 
-        def pick(name, window, held, dtype):
+        def pick(name, table, offsets, dtype):
             picked = tile(name, [P, S], dtype)
-            nc.vector.tensor_copy(picked[:], window.indirect(held[:]))
+            nc.vector.tensor_copy(picked[:], table.indirect(offsets[:]))
             return picked
 
         def deal(name, picked, dtype):
@@ -94,134 +104,124 @@ def tile_picked_cdjoinsoftbhopb_none_p_kernel(
             )
             return dealt
 
+        def round_and_deal(copy, grouped, raw, columns):
+            copy(
+                grouped[:, :, columns.start // PACK : columns.stop // PACK, :].rearrange("p t m j -> p m j t"),
+                raw.rearrange("p j (m t) -> p m j t", t=PACK),
+            )
+
         def quantise(name, grouped, width):
             codes = tile(name + "_codes", [P, width], U32)
             scales = tile(name + "_scales", [P, width], U8)
             nc.vector.quantize_mx(out=codes[:].bitcast(FP8X4), scales=scales[:], in_=grouped)
             return codes, scales
 
-        def product(acc, lhs, t, rhs):
-            m = slice(t * P, (t + 1) * P)
+        def product(acc, stationary, t, moving):
+            columns = slice(t * P, (t + 1) * P)
             nc.tensor.matmul_mx(
-                out=acc, lhsT=lhs[0][:, m].bitcast(FP8X4), lhsT_scale=lhs[1][:, m],
-                rhs=rhs[0][:].bitcast(FP8X4), rhs_scale=rhs[1][:], start=True, stop=True,
+                out=acc,
+                lhsT=stationary[0][:, columns].bitcast(FP8X4),
+                lhsT_scale=stationary[1][:, columns],
+                rhs=moving[0][:].bitcast(FP8X4),
+                rhs_scale=moving[1][:],
+                start=True,
+                stop=True,
             )
 
-        def planes(name, dtype=F32):
-            return [tile("%s%d" % (name, t), [P, S], dtype) for t in range(PACK)]
-
-        xo_bytes = pick("xo_bytes", x_bytes[:], offs_l, U8)
-        xt_bytes = pick("xt_bytes", x_bytes[:], two_l, U8)
+        x_offs_bytes = pick("x_offs_bytes", x_bytes[:], offs_list, U8)
+        x_two_bytes = pick("x_two_bytes", x_bytes[:], two_list, U8)
         w1_grouped = tile("w1_grouped", [P, PACK, P, PACK], BF16)
         for h in range(2):
-            nc.scalar.copy(
-                w1_grouped[:, :, h * 64 : (h + 1) * 64, :].rearrange("p t m j -> p m j t"),
-                w1_raw[h][:].rearrange("p j (m t) -> p m j t", t=PACK),
-            )
-        w1_q = quantise("w1", w1_grouped[:].rearrange("p t m j -> p (t m j)"), S)
-        xo_words = pick("xo_words", x_table[:].bitcast(U32), offs_l, U32)
-        dk_bytes = pick("dk_bytes", d_bytes[:], k1_l, U8)
-        xt_words = pick("xt_words", x_table[:].bitcast(U32), two_l, U32)
-        dealt_bytes = deal("dealt_bytes", dk_bytes, U8)
+            round_and_deal(nc.scalar.copy, w1_grouped, w1_raw[h][:], half(h))
+        w1_mx = quantise("w1", w1_grouped[:].rearrange("p t m j -> p (t m j)"), S)
+        x_offs_words = pick("x_offs_words", x_table[:].bitcast(U32), offs_list, U32)
+        d_picked_bytes = pick("d_picked_bytes", d_bytes[:], k1_list, U8)
+        x_two_words = pick("x_two_words", x_table[:].bitcast(U32), two_list, U32)
+        d_dealt_bytes = deal("d_dealt_bytes", d_picked_bytes, U8)
         for e in range(2):
-            nc.sync.dma_start(dealt_bytes[2 + e : P : 32, :].bitcast(I32), dealt_bytes[16 + e : P : 32, :].bitcast(I32))
-
+            nc.sync.dma_start(
+                d_dealt_bytes[2 + e : P : QUADRANT, :].bitcast(I32),
+                d_dealt_bytes[GROUP + e : P : QUADRANT, :].bitcast(I32),
+            )
         w2_grouped = tile("w2_grouped", [P, PACK, P, PACK], BF16)
-        nc.scalar.copy(
-            w2_grouped[:, :, 0 : EARLY // PACK, :].rearrange("p t m j -> p m j t"),
-            w2_early[:, :, 0:EARLY].rearrange("p j (m t) -> p m j t", t=PACK),
-        )
-        y_n1, diff = planes("y_n1"), planes("diff")
-        y = [staged.tile([P, S], F32, name="y%d" % t, align_bytes=64, offset=t * S * 4) for t in range(PACK)]
-        st2 = [shared.tile([P, S], F32, name="st2_%d" % t, align_bytes=64, offset=t * S * 4) for t in range(PACK)]
-        z_planes = tile("z_planes", [P, PACK, S], BF16)
+        round_and_deal(nc.scalar.copy, w2_grouped, w2_first[:, :, 0:W2_ON_SCALAR], slice(0, W2_ON_SCALAR))
 
-        y_acc = [psum.tile([P, S], F32, name="ya_acc%d" % t) for t in range(PACK)]
+        twice_y_n1, diff = planes("twice_y_n1_", S), planes("diff", S)
+        y = windows(w2_then_y, "y")
+        twice_st = windows(d_then_st, "twice_st")
+        z_planes = tile("z_planes", [P, PACK, S], BF16)
+        y_acc = [psum.tile([P, S], F32, name="y_then_a%d" % t) for t in range(PACK)]
 
         def project(t):
-            product(y_acc[t][:], w1_q, t, (xo_words, xo_bytes))
-            nc.scalar.copy(y[t][:], y_acc[t][:])
-
-        def fetch_n1(t):
-            for h in range(2):
-                nc.scalar.activation(y_n1[t][:, cols(h)], y[t][:].indirect(half_list(n1_l, h)), ACT.Copy, scale=2.0)
+            product(y_acc[t][:], w1_mx, t, (x_offs_words, x_offs_bytes))
+            nc.scalar.copy(y[t][:, 0:S], y_acc[t][:])
 
         def larger(t):
-            nc.vector.scalar_tensor_tensor(st2[t][:], y_acc[t][:], 2.0, y_n1[t][:], ALU.mult, ALU.max)
+            nc.vector.scalar_tensor_tensor(twice_st[t][:, 0:S], y_acc[t][:], 2.0, twice_y_n1[t][:], ALU.mult, ALU.max)
 
-        def fetch_n2(t, h):
-            nc.vector.tensor_tensor(
-                diff[t][:, cols(h)], st2[t][:].indirect(half_list(n2_l, h)), y[t][:, cols(h)], ALU.subtract
-            )
+        def fetch_n2(t):
+            nc.vector.tensor_tensor(diff[t][:], twice_st[t][:].indirect(n2_list[:]), y[t][:, 0:S], ALU.subtract)
 
-        def apply_gain(t, c):
-            nc.vector.tensor_scalar(z_planes[:, t, c], diff[t][:, c], gain[:, t : t + 1], 0.5, ALU.mult, ALU.mult)
+        def apply_gain(t):
+            nc.vector.tensor_scalar(z_planes[:, t, :], diff[t][:], gain[:, t : t + 1], 0.5, ALU.mult, ALU.mult)
 
         project(0)
         for t in range(PACK):
             if t + 1 < PACK:
                 project(t + 1)
-            fetch_n1(t)
+            nc.scalar.activation(twice_y_n1[t][:], y[t][:].indirect(n1_list[:]), ACT.Copy, scale=2.0)
 
-        dk_words = pick("dk_words", d_table[:].bitcast(U32), k1_l, U32)
+        d_picked_words = pick("d_picked_words", d_table[:].bitcast(U32), k1_list, U32)
         larger(0)
-        dealt_words = deal("dealt_words", dk_words, U32)
-        fetch_n2(0, 0)
-        fetch_n2(0, 1)
+        d_dealt_words = deal("d_dealt_words", d_picked_words, U32)
+        fetch_n2(0)
         for t in range(1, PACK):
             larger(t)
-            apply_gain(t - 1, slice(0, S))
-            fetch_n2(t, 0)
-            fetch_n2(t, 1)
-        nc.vector.tensor_copy(
-            w2_grouped[:, :, EARLY // PACK : P, :].rearrange("p t m j -> p m j t"),
-            w2_late[:].rearrange("p j (m t) -> p m j t", t=PACK),
-        )
-        apply_gain(PACK - 1, slice(0, S))
-        w2_q = quantise("w2", w2_grouped[:].rearrange("p t m j -> p (t m j)"), S)
+            apply_gain(t - 1)
+            fetch_n2(t)
+        round_and_deal(nc.vector.tensor_copy, w2_grouped, w2_rest[:], slice(W2_ON_SCALAR, S))
+        apply_gain(PACK - 1)
+        w2_mx = quantise("w2", w2_grouped[:].rearrange("p t m j -> p (t m j)"), S)
         z_grouped = [tile("z_grouped%d" % h, [P, HALF, PACK], BF16) for h in range(2)]
         for h in range(2):
             nc.vector.tensor_copy(
                 z_grouped[h][:].rearrange("p (c i) t -> p c t i", i=4),
-                z_planes[:, :, cols(h)].rearrange("p t (c i) -> p c t i", i=4),
+                z_planes[:, :, half(h)].rearrange("p t (c i) -> p c t i", i=4),
             )
-        z_q = [quantise("z%d" % h, z_grouped[h][:].rearrange("p c t -> p (c t)"), HALF) for h in range(2)]
+        z_mx = [quantise("z%d" % h, z_grouped[h][:].rearrange("p c t -> p (c t)"), HALF) for h in range(2)]
 
-        b, tanh_b, b_n4, mix, a = planes("b"), planes("tanh_b"), planes("b_n4"), planes("mix"), planes("a")
+        tanh_b, b_n4, mix = planes("tanh_b", S), planes("b_n4_", S), planes("mix", S)
+        b, a = planes("b", WINDOW), planes("a", WINDOW)
         for t in range(PACK):
             b_acc = psum.tile([P, S], F32, name="b_acc%d" % t)
-            product(b_acc[:], (dealt_words, dealt_bytes), t, (xt_words, xt_bytes))
-            nc.scalar.activation(b[t][:], b_acc[:], ACT.Copy, scale=0.0625)
+            product(b_acc[:], (d_dealt_words, d_dealt_bytes), t, (x_two_words, x_two_bytes))
+            nc.scalar.activation(b[t][:, 0:S], b_acc[:], ACT.Copy, scale=0.0625)
             nc.scalar.activation(tanh_b[t][:], b_acc[:], ACT.Tanh, scale=0.0625)
-            plain = [h for h in range(2) if 2 * t + h < 5]
-            for h in range(2):
-                if h in plain:
-                    nc.scalar.activation(b_n4[t][:, cols(h)], b[t][:].indirect(half_list(n4_l, h)), ACT.Copy)
-            if plain:
-                span = slice(0, HALF * len(plain))
-                nc.vector.tensor_tensor(mix[t][:, span], b_n4[t][:, span], tanh_b[t][:, span], ALU.mult)
-            for h in range(2):
-                if h not in plain:
-                    nc.vector.tensor_tensor(
-                        mix[t][:, cols(h)], b[t][:].indirect(half_list(n4_l, h)), tanh_b[t][:, cols(h)], ALU.mult
-                    )
+            nc.scalar.activation(b_n4[t][:], b[t][:].indirect(n4_list[:]), ACT.Copy)
+            nc.vector.tensor_tensor(mix[t][:], b_n4[t][:], tanh_b[t][:], ALU.mult)
 
         for t in range(PACK):
-            a_acc = psum.tile([P, S], F32, name="ya_acc%d" % t)
+            a_acc = psum.tile([P, S], F32, name="y_then_a%d" % t)
             for h in range(2):
-                product(a_acc[:, cols(h)], w2_q, t, z_q[h])
-            nc.scalar.copy(a[t][:], a_acc[:])
+                product(a_acc[:, half(h)], w2_mx, t, z_mx[h])
+            nc.scalar.copy(a[t][:, 0:S], a_acc[:])
 
-        out_rows = out.rearrange("(p t) j -> t p j", t=PACK)
+        out_planes = out.rearrange("(p t) j -> t p j", t=PACK)
+
+        def finish(t, columns, fused):
+            width = columns.stop - columns.start
+            a_n3 = a[t][:].indirect(n3_list[:, columns.start // GROUP : columns.stop // GROUP])
+            result = tile("result%d_%d" % (t, columns.start), [P, width], F32)
+            if not fused:
+                fetched = tile("fetched%d_%d" % (t, columns.start), [P, width], F32)
+                nc.scalar.activation(fetched[:], a_n3, ACT.Copy)
+                a_n3 = fetched[:]
+            nc.vector.tensor_tensor(result[:], a_n3, mix[t][:, columns], ALU.subtract)
+            nc.sync.dma_start(out_planes[t][:, columns], result[:])
+
         for t in range(PACK):
-            for h in range(2):
-                result = tile("result%d_%d" % (t, h), [P, HALF], F32)
-                if 2 * t + h < 4:
-                    nc.vector.tensor_tensor(
-                        result[:], a[t][:].indirect(half_list(n3_l, h)), mix[t][:, cols(h)], ALU.subtract
-                    )
-                else:
-                    a_n3 = tile("a_n3_%d_%d" % (t, h), [P, HALF], F32)
-                    nc.scalar.activation(a_n3[:], a[t][:].indirect(half_list(n3_l, h)), ACT.Copy)
-                    nc.vector.tensor_tensor(result[:], a_n3[:], mix[t][:, cols(h)], ALU.subtract)
-                nc.sync.dma_start(out_rows[t][:, cols(h)], result[:])
+            if 2 * t + 2 <= FUSED_HALVES:
+                finish(t, slice(0, S), True)
+            else:
+                for h in range(2):
+                    finish(t, half(h), 2 * t + h < FUSED_HALVES)

from contextlib import ExitStack

import concourse.mybir as mybir

F32 = mybir.dt.float32
BF16 = mybir.dt.bfloat16
I32 = mybir.dt.int32
U32 = mybir.dt.uint32
U16 = mybir.dt.uint16
U8 = mybir.dt.uint8
FP8X4 = mybir.dt.float8_e4m3fn_x4
ALU = mybir.AluOpType
ACT = mybir.ActivationFunctionType

P = 128
PACK = 4
S = 512
T = 2048
HALF = S // 2
GROUP = 16
QUADRANT = 32
BLOCKS = 16
F32_BYTES = 4
WINDOW = 2 * S
W2_ON_SCALAR = 192
FUSED_HALVES = 5
FLOPS = 3 * 2 * 512 * 512 * 512


def tile_picked_cdjoinsoftbhopb_none_p_kernel(
    tc, x_words, x_scales, w1, gn, w2, d_words, d_scales, offs, n1, n2, two, k1, n3, n4, out
):
    nc = tc.nc
    with ExitStack() as ctx:
        keep = ctx.enter_context(tc.tile_pool(name="keep", bufs=1))
        d_then_st = ctx.enter_context(tc.tile_pool(name="d_then_st", bufs=1))
        w2_then_y = ctx.enter_context(tc.tile_pool(name="w2_then_y", bufs=1))
        psum = ctx.enter_context(tc.psum_pool(name="psum", bufs=1))

        def tile(name, shape, dtype):
            return keep.tile(shape, dtype, name=name, align_bytes=64)

        def planes(name, width):
            return [tile("%s%d" % (name, t), [P, width], F32) for t in range(PACK)]

        def windows(pool, name):
            return [
                pool.tile([P, WINDOW], F32, name="%s%d" % (name, t), align_bytes=64, offset=t * WINDOW * F32_BYTES)
                for t in range(PACK)
            ]

        def half(h):
            return slice(h * HALF, (h + 1) * HALF)

        def load_list(name, source):
            offsets = tile(name, [P, S // GROUP], U16)
            nc.sync.dma_start(offsets[:], source)
            return offsets

        def as_words(packed):
            return packed[0].rearrange("p n r -> p (n r)").bitcast(I32)

        x_bytes = tile("x_bytes", [P, T], U8)
        d_bytes = tile("d_bytes", [P, T], U8)
        nc.vector.memset(x_bytes[:].bitcast(I32), 0)
        nc.vector.memset(d_bytes[:].bitcast(I32), 0)

        offs_list = load_list("offs_list", offs)
        w1_rows = w1.rearrange("(p j) c -> p j c", j=PACK)
        w1_raw = [tile("w1_raw%d" % h, [P, PACK, HALF], F32) for h in range(2)]
        nc.sync.dma_start(w1_raw[0][:], w1_rows[:, :, half(0)])
        for s in range(PACK):
            nc.sync.dma_start(x_bytes[s:P:QUADRANT, :].bitcast(I32), x_scales[0, s:BLOCKS:PACK, :].bitcast(I32))
        two_list = load_list("two_list", two)
        nc.sync.dma_start(w1_raw[1][:], w1_rows[:, :, half(1)])
        x_table = tile("x_table", [P, T], I32)
        nc.sync.dma_start(x_table[:], as_words(x_words))
        k1_list = load_list("k1_list", k1)
        for e in range(2):
            nc.sync.dma_start(d_bytes[e:P:GROUP, :].bitcast(I32), d_scales[0, e:BLOCKS:2, :].bitcast(I32))
        n1_list = load_list("n1_list", n1)
        w2_rows = w2.rearrange("(p j) c -> p j c", j=PACK)
        w2_first = w2_then_y.tile([P, PACK, WINDOW], F32, name="w2_first", align_bytes=64, offset=0)
        nc.sync.dma_start(w2_first[:, :, 0:W2_ON_SCALAR], w2_rows[:, :, 0:W2_ON_SCALAR])
        d_table = d_then_st.tile([P, T], I32, name="d_table", align_bytes=64, offset=S * F32_BYTES)
        nc.sync.dma_start(d_table[:], as_words(d_words))
        n2_list = load_list("n2_list", n2)
        gain = tile("gain", [P, PACK], F32)
        nc.sync.dma_start(gain[:], gn.rearrange("(p t) o -> p (t o)", t=PACK))
        w2_rest = tile("w2_rest", [P, PACK, S - W2_ON_SCALAR], F32)
        nc.sync.dma_start(w2_rest[:], w2_rows[:, :, W2_ON_SCALAR:S])
        n4_list = load_list("n4_list", n4)
        n3_list = load_list("n3_list", n3)

        def pick(name, table, offsets, dtype):
            picked = tile(name, [P, S], dtype)
            nc.vector.tensor_copy(picked[:], table.indirect(offsets[:]))
            return picked

        def deal(name, picked, dtype):
            dealt = tile(name, [P, S], dtype)
            nc.vector.tensor_copy(
                dealt[:].rearrange("p (t m) -> p m t", t=PACK), picked[:].rearrange("p (m t) -> p m t", t=PACK)
            )
            return dealt

        def round_and_deal(copy, grouped, raw, columns):
            copy(
                grouped[:, :, columns.start // PACK : columns.stop // PACK, :].rearrange("p t m j -> p m j t"),
                raw.rearrange("p j (m t) -> p m j t", t=PACK),
            )

        def quantise(name, grouped, width):
            codes = tile(name + "_codes", [P, width], U32)
            scales = tile(name + "_scales", [P, width], U8)
            nc.vector.quantize_mx(out=codes[:].bitcast(FP8X4), scales=scales[:], in_=grouped)
            return codes, scales

        def product(acc, stationary, t, moving):
            columns = slice(t * P, (t + 1) * P)
            nc.tensor.matmul_mx(
                out=acc,
                lhsT=stationary[0][:, columns].bitcast(FP8X4),
                lhsT_scale=stationary[1][:, columns],
                rhs=moving[0][:].bitcast(FP8X4),
                rhs_scale=moving[1][:],
                start=True,
                stop=True,
            )

        x_offs_bytes = pick("x_offs_bytes", x_bytes[:], offs_list, U8)
        x_two_bytes = pick("x_two_bytes", x_bytes[:], two_list, U8)
        w1_grouped = tile("w1_grouped", [P, PACK, P, PACK], BF16)
        for h in range(2):
            round_and_deal(nc.scalar.copy, w1_grouped, w1_raw[h][:], half(h))
        w1_mx = quantise("w1", w1_grouped[:].rearrange("p t m j -> p (t m j)"), S)
        x_offs_words = pick("x_offs_words", x_table[:].bitcast(U32), offs_list, U32)
        d_picked_bytes = pick("d_picked_bytes", d_bytes[:], k1_list, U8)
        x_two_words = pick("x_two_words", x_table[:].bitcast(U32), two_list, U32)
        d_dealt_bytes = deal("d_dealt_bytes", d_picked_bytes, U8)
        for e in range(2):
            nc.sync.dma_start(
                d_dealt_bytes[2 + e : P : QUADRANT, :].bitcast(I32),
                d_dealt_bytes[GROUP + e : P : QUADRANT, :].bitcast(I32),
            )
        w2_grouped = tile("w2_grouped", [P, PACK, P, PACK], BF16)
        round_and_deal(nc.scalar.copy, w2_grouped, w2_first[:, :, 0:W2_ON_SCALAR], slice(0, W2_ON_SCALAR))

        twice_y_n1, diff = planes("twice_y_n1_", S), planes("diff", S)
        y = windows(w2_then_y, "y")
        twice_st = windows(d_then_st, "twice_st")
        z_planes = tile("z_planes", [P, PACK, S], BF16)
        y_acc = [psum.tile([P, S], F32, name="y_then_a%d" % t) for t in range(PACK)]

        def project(t):
            product(y_acc[t][:], w1_mx, t, (x_offs_words, x_offs_bytes))
            nc.scalar.copy(y[t][:, 0:S], y_acc[t][:])

        def larger(t):
            nc.vector.scalar_tensor_tensor(twice_st[t][:, 0:S], y_acc[t][:], 2.0, twice_y_n1[t][:], ALU.mult, ALU.max)

        def fetch_n2(t):
            nc.vector.tensor_tensor(diff[t][:], twice_st[t][:].indirect(n2_list[:]), y[t][:, 0:S], ALU.subtract)

        def apply_gain(t):
            nc.vector.tensor_scalar(z_planes[:, t, :], diff[t][:], gain[:, t : t + 1], 0.5, ALU.mult, ALU.mult)

        project(0)
        for t in range(PACK):
            if t + 1 < PACK:
                project(t + 1)
            nc.scalar.activation(twice_y_n1[t][:], y[t][:].indirect(n1_list[:]), ACT.Copy, scale=2.0)

        d_picked_words = pick("d_picked_words", d_table[:].bitcast(U32), k1_list, U32)
        larger(0)
        d_dealt_words = deal("d_dealt_words", d_picked_words, U32)
        fetch_n2(0)
        for t in range(1, PACK):
            larger(t)
            apply_gain(t - 1)
            fetch_n2(t)
        round_and_deal(nc.vector.tensor_copy, w2_grouped, w2_rest[:], slice(W2_ON_SCALAR, S))
        apply_gain(PACK - 1)
        w2_mx = quantise("w2", w2_grouped[:].rearrange("p t m j -> p (t m j)"), S)
        z_grouped = [tile("z_grouped%d" % h, [P, HALF, PACK], BF16) for h in range(2)]
        for h in range(2):
            nc.vector.tensor_copy(
                z_grouped[h][:].rearrange("p (c i) t -> p c t i", i=4),
                z_planes[:, :, half(h)].rearrange("p t (c i) -> p c t i", i=4),
            )
        z_mx = [quantise("z%d" % h, z_grouped[h][:].rearrange("p c t -> p (c t)"), HALF) for h in range(2)]

        tanh_b, b_n4, mix = planes("tanh_b", S), planes("b_n4_", S), planes("mix", S)
        b, a = planes("b", WINDOW), planes("a", WINDOW)
        for t in range(PACK):
            b_acc = psum.tile([P, S], F32, name="b_acc%d" % t)
            product(b_acc[:], (d_dealt_words, d_dealt_bytes), t, (x_two_words, x_two_bytes))
            nc.scalar.activation(b[t][:, 0:S], b_acc[:], ACT.Copy, scale=0.0625)
            nc.scalar.activation(tanh_b[t][:], b_acc[:], ACT.Tanh, scale=0.0625)
            nc.scalar.activation(b_n4[t][:], b[t][:].indirect(n4_list[:]), ACT.Copy)
            nc.vector.tensor_tensor(mix[t][:], b_n4[t][:], tanh_b[t][:], ALU.mult)

        for t in range(PACK):
            a_acc = psum.tile([P, S], F32, name="y_then_a%d" % t)
            for h in range(2):
                product(a_acc[:, half(h)], w2_mx, t, z_mx[h])
            nc.scalar.copy(a[t][:, 0:S], a_acc[:])

        out_planes = out.rearrange("(p t) j -> t p j", t=PACK)

        def finish(t, columns, fused):
            width = columns.stop - columns.start
            a_n3 = a[t][:].indirect(n3_list[:, columns.start // GROUP : columns.stop // GROUP])
            result = tile("result%d_%d" % (t, columns.start), [P, width], F32)
            if not fused:
                fetched = tile("fetched%d_%d" % (t, columns.start), [P, width], F32)
                nc.scalar.activation(fetched[:], a_n3, ACT.Copy)
                a_n3 = fetched[:]
            nc.vector.tensor_tensor(result[:], a_n3, mix[t][:, columns], ALU.subtract)
            nc.sync.dma_start(out_planes[t][:, columns], result[:])

        for t in range(PACK):
            if 2 * t + 2 <= FUSED_HALVES:
                finish(t, slice(0, S), True)
            else:
                for h in range(2):
                    finish(t, half(h), 2 * t + h < FUSED_HALVES)
